import numpy as np
import ml_dtypes


def mxq(x, axis, fmt="e4m3"):
    dtype, down = {"e4m3": (ml_dtypes.float8_e4m3fn, 7), "e5m2": (ml_dtypes.float8_e5m2, 14)}[fmt]
    v = np.moveaxis(np.asarray(x, np.float32).astype(ml_dtypes.bfloat16).astype(np.float64), axis, -1)
    blocks = v.reshape(v.shape[:-1] + (-1, 32))
    amax = np.abs(blocks).max(-1, keepdims=True)
    byte = np.maximum(np.where(amax > 0, np.frexp(amax)[1] - 1 + 127, 0) - down, 1)
    scale = np.exp2(byte - 127.0)
    codes = (blocks / scale).astype(np.float32).astype(dtype).astype(np.float64)
    return np.moveaxis((codes * scale).reshape(v.shape), -1, axis)


WIDE = False


def mx_kscale(k):
    if not WIDE:
        return np.ones(k)
    levels = np.array([10, -10, 5, -5, 0])
    if k % 512:
        return np.exp2(np.random.permutation(np.resize(levels, k // 32))).repeat(32)
    a = np.empty((k // 512, 16))
    for p in range(k // 512):
        a[p, :8] = np.random.permutation(np.resize(levels, 8))
        for g in range(8):
            far = levels[np.abs(levels - a[p, g]) >= 10]
            a[p, g + 8] = far[np.random.randint(len(far))]
    return np.exp2(a.ravel()).repeat(32)


BF16 = ml_dtypes.bfloat16


def bf(x):
    return np.asarray(x, np.float32).astype(BF16)


def f64(x):
    return np.asarray(x).astype(np.float64)


E2M1 = np.array([0.0, 0.5, 1.0, 1.5, 2.0, 3.0, 4.0, 6.0, -0.0, -0.5, -1.0, -1.5, -2.0, -3.0, -4.0, -6.0])


def pack_weight(w, fmt):
    k, n = w.shape
    w = f64(bf(w)).reshape(k // 32, 32, n)
    amax = np.abs(w).max(1)
    if fmt == "e4m3":
        byte = np.frexp(amax)[1] - 1 + 127 - 7
    else:
        mant, ex = np.frexp(amax / 6.0)
        byte = np.where(mant > 0.5, ex, ex - 1) + 127
    byte = np.clip(np.where(amax > 0, byte, 1), 1, 254)
    scaled = (w * np.exp2(127.0 - byte)[:, None, :]).reshape(k, n).astype(np.float32)
    by_word = np.ascontiguousarray(scaled.reshape(k // 512, 128, 4, n).transpose(0, 1, 3, 2))
    if fmt == "e4m3":
        words = by_word.astype(ml_dtypes.float8_e4m3fn).view(np.uint8)
    else:
        c = by_word.astype(ml_dtypes.float4_e2m1fn).view(np.uint8) & 0xF
        words = c[..., 0::2] | (c[..., 1::2] << 4)
    return np.ascontiguousarray(words), np.ascontiguousarray(byte.astype(np.uint8).reshape(k // 512, 16, n))


def unpack_weight(words, scales, fmt):
    g, p, n, _ = words.shape
    if fmt == "e4m3":
        vals = np.ascontiguousarray(words).view(ml_dtypes.float8_e4m3fn).astype(np.float64)
    else:
        nib = np.empty((g, p, n, 4), np.uint8)
        nib[..., 0::2] = words & 0xF
        nib[..., 1::2] = words >> 4
        vals = E2M1[nib]
    vals = vals * np.repeat(np.exp2(scales.astype(np.float64) - 127.0), 8, axis=1)[..., None]
    return vals.transpose(0, 1, 3, 2).reshape(g * 512, n)
def pack4(w):
    words, scales = pack_weight(w, "e2m1")
    return words.reshape(words.shape[0], 128, -1), scales


def unpack4(words, scales):
    return unpack_weight(words.reshape(words.shape[0], 128, -1, 2), scales, "e2m1")


def planes(Y):
    n, m = Y.shape
    b = f64(bf(Y)).reshape(n // 32, 32, m)
    amax = np.abs(b).max(1)
    byte = np.clip(np.where(amax > 0, np.frexp(amax)[1] - 1 + 127 - 7, 1), 1, 254)
    codes = (b * np.exp2(127.0 - byte)[:, None, :]).reshape(n, m).astype(np.float32).astype(ml_dtypes.float8_e4m3fn).view(np.uint8)
    words = codes.reshape(n // 512, 128, 4, m).transpose(0, 1, 3, 2)
    return np.ascontiguousarray(words), np.ascontiguousarray(byte.astype(np.uint8).reshape(n // 512, 16, m))


TGT, SRC, F, D, DIM = 2048, 1536, 1024, 512, 3
SIGMA2, OUTLIER = 0.8, 0.1

def setup_inputs():
    rn = np.random.randn
    tgt, src = rn(TGT, DIM), rn(SRC, DIM)
    e = np.exp(-((tgt[:, None, :] - src[None, :, :]) ** 2).sum(2) / (2.0 * SIGMA2))
    c = (2.0 * np.pi * SIGMA2) ** (DIM / 2.0) * OUTLIER / (1.0 - OUTLIER) * SRC / TGT
    P = e / (e.sum(1, keepdims=True) + c)
    mass = P.sum(0)
    omega, phase = rn(DIM, F), 2.0 * np.pi * np.random.rand(F)
    proj = (tgt[:, :, None] * omega[None, :, :]).sum(1)
    X = np.sqrt(2.0) * np.sin(proj + phase) + 0.3 * rn(TGT, F)
    s, t = mx_kscale(TGT), mx_kscale(F)
    p_words, p_scales = pack4(P * s[:, None])
    x_words, x_scales = pack4(X / s[:, None] * t[None, :])
    return {"p_words": p_words, "p_scales": p_scales,
            "x_words": x_words, "x_scales": x_scales,
            "mass": bf(mass),
            "proj_w": bf(1.5 * rn(F, D) / np.sqrt(F) / t[:, None]),
            "bias": bf(0.3 * rn(D)),
            "src_feat": bf(0.8 * rn(SRC, D)),
            "point_weight": bf(np.exp(0.8 * rn(SRC)))}

def reference(p_words, p_scales, x_words, x_scales, mass, proj_w, bias, src_feat, point_weight):
    P = unpack4(p_words, p_scales)
    X = unpack4(x_words, x_scales)
    h = (P.T @ X) / f64(mass)[:, None]
    z = mxq(h, 1, "e4m3") @ mxq(f64(proj_w), 0, "e4m3")
    y = (z + f64(bias) - f64(src_feat)) * f64(point_weight)[:, None]
    Y = y.reshape(SRC, D)
    words, scales = planes(Y)
    return y, words, scales

@@ -1,0 +1,355 @@
+from contextlib import ExitStack
+
+import concourse.mybir as mybir
+from concourse.masks import make_identity
+
+TGT, SRC, F, D = 2048, 1536, 1024, 512
+FLOPS = 2 * TGT * SRC * F + 2 * SRC * F * D
+
+F32 = mybir.dt.float32
+BF16 = mybir.dt.bfloat16
+I32 = mybir.dt.int32
+U32 = mybir.dt.uint32
+U8 = mybir.dt.uint8
+FP4X4 = mybir.dt.float4_e2m1fn_x4
+FP8X4 = mybir.dt.float8_e4m3fn_x4
+ALU = mybir.AluOpType
+ACT = mybir.ActivationFunctionType
+
+P = 128
+PACK = 4
+CHUNK = P * PACK
+NCH = SRC // CHUNK
+TP = TGT // CHUNK
+FP = F // CHUNK
+HALF = CHUNK // 2
+HM = HALF // PACK
+QUADS = 4
+
+
+def tile_drift_mass_residual_k5_kernel(
+    tc, p_words, p_scales, x_words, x_scales, mass, proj_w, bias, src_feat, point_weight, out_0, out_1, out_2
+):
+    nc = tc.nc
+    with ExitStack() as ctx:
+        keep = ctx.enter_context(tc.tile_pool(name="keep", bufs=1))
+        work = ctx.enter_context(tc.tile_pool(name="work", bufs=2))
+        psum = ctx.enter_context(tc.psum_pool(name="psum", bufs=8))
+        ctx.enter_context(tc.manual_schedule())
+
+        def kept(name, shape, dtype):
+            return keep.tile(shape, dtype, name=name, align_bytes=256)
+
+        def bank(name):
+            return psum.tile([P, CHUNK], F32, name=name, tag="bank")
+
+        x_raw = [kept("x_raw%d" % g, [P, 2 * F], U8) for g in range(TP)]
+        x_code = [kept("x_code%d" % g, [P, 2 * F], U8) for g in range(TP)]
+        xs_raw = kept("xs_raw", [P, TP, F], U8)
+        x_scale = [kept("x_scale%d" % g, [P, F], U8) for g in range(TP)]
+        p_first = [kept("p_first%d" % i, [P, 2, 2 * CHUNK], U8) for i in range(2)]
+        p_rest = [kept("p_rest%d" % c, [P, TP, 2 * CHUNK], U8) for c in range(NCH - 1)]
+        ps_first = kept("ps_first", [P, TP, CHUNK], U8)
+        ps_rest = kept("ps_rest", [P, TP, SRC - CHUNK], U8)
+        w_raw = [kept("w_raw%d" % G, [P, PACK, D], BF16) for G in range(FP)]
+        w_group = [kept("w_group%d" % G, [P, D, PACK], BF16) for G in range(FP)]
+        w_code = [kept("w_code%d" % G, [P, D], U32) for G in range(FP)]
+        w_scale = [kept("w_scale%d" % G, [P, D], U8) for G in range(FP)]
+        mass_col = kept("mass_col", [P, NCH, PACK], BF16)
+        rmass_col = kept("rmass_col", [P, NCH * PACK], F32)
+        rmass = [kept("rmass%d" % c, [P, PACK, P], F32) for c in range(NCH)]
+        weight_raw = kept("weight_raw", [P, NCH, PACK], BF16)
+        weight_col = kept("weight_col", [P, NCH * PACK], F32)
+        bias_row = kept("bias_row", [P, D], BF16)
+        feat = [kept("feat%d" % c, [P, PACK, D], BF16) for c in range(NCH)]
+        offset = [[kept("offset%d_%d" % (c, t), [P, D], F32) for t in range(PACK)] for c in range(NCH)]
+        h_code = [[kept("h_code%d_%d" % (c, G), [P, CHUNK], U32) for G in range(FP)] for c in range(NCH)]
+        h_scale = [[kept("h_scale%d_%d" % (c, G), [P, CHUNK], U8) for G in range(FP)] for c in range(NCH)]
+        y_code = [kept("y_code%d" % c, [P, D], U32) for c in range(NCH)]
+        y_scale = [kept("y_scale%d" % c, [P, D], U8) for c in range(NCH)]
+        ident = kept("ident", [P, P], F32)
+
+        def p_code(c, g):
+            return p_first[g // 2][:, g % 2, :] if c == 0 else p_rest[c - 1][:, g, :]
+
+        def p_scale(c, g):
+            return ps_first[:, g, :] if c == 0 else ps_rest[:, g, (c - 1) * CHUNK : c * CHUNK]
+
+        def load_scale_rows(plane, rows):
+            for q in range(QUADS):
+                nc.sync.dma_start(
+                    out=plane[32 * q : 32 * q + 4, :, :].bitcast(I32),
+                    in_=rows[:, 4 * q : 4 * q + 4, :].rearrange("g r n -> r g n").bitcast(I32),
+                )
+
+        def load_p_words(dst, gs, c):
+            cols = slice(2 * CHUNK * c, 2 * CHUNK * (c + 1))
+            nc.sync.dma_start(out=dst[:].bitcast(I32), in_=p_words[gs, :, cols].rearrange("g p n -> p g n").bitcast(I32))
+
+        def load_x_words(g):
+            nc.sync.dma_start(out=x_raw[g][:].bitcast(I32), in_=x_words[g].bitcast(I32))
+
+        def load_feat(c):
+            rows = src_feat[CHUNK * c : CHUNK * (c + 1), :]
+            nc.sync.dma_start(out=feat[c][:], in_=rows.rearrange("(p t) d -> p t d", t=PACK))
+
+        def sort_x_words(g):
+            nc.vector.tensor_copy(
+                out=x_code[g][:].bitcast(I32).rearrange("p (j q w) -> p j q w", j=8, w=4),
+                in_=x_raw[g][:].bitcast(I32).rearrange("p (q j w) -> p j q w", j=8, w=4),
+            )
+
+        def sort_x_scales(g):
+            nc.vector.tensor_copy(
+                out=x_scale[g][:].bitcast(I32).rearrange("p (j q w) -> p j q w", j=8, w=2),
+                in_=xs_raw[:, g, :].bitcast(I32).rearrange("p (q j w) -> p j q w", j=8, w=2),
+            )
+
+        def interleave(engine_copy, dst, src):
+            engine_copy(
+                out=dst.rearrange("p (c i) t -> p c t i", i=4),
+                in_=src.rearrange("p t (c i) -> p c t i", i=4),
+            )
+
+        def quantize(codes, scales, grouped):
+            nc.vector.quantize_mx(out=codes.bitcast(FP8X4), scales=scales, in_=grouped.rearrange("p n t -> p (n t)"))
+
+        def group_w(G, half):
+            cols = slice(HALF * half, HALF * (half + 1))
+            interleave(nc.scalar.copy, w_group[G][:, cols, :], w_raw[G][:, :, cols])
+
+        def quantize_w(G):
+            quantize(w_code[G][:], w_scale[G][:], w_group[G][:])
+
+        sums = {}
+        pairs = {}
+        h_group = {}
+        z_bank = {}
+        y_tile = {}
+        y_group = {}
+
+        def split(b):
+            return b // 4, (b // 2) % 2, b % 2
+
+        def first_pass(c, b, e, g):
+            G, half, u = split(b)
+            j = PACK * G + 2 * u + e
+            if (c, b) not in sums:
+                sums[c, b] = bank("sums%d_%d" % (c, b))
+            nc.tensor.matmul_mx(
+                out=sums[c, b][:, HALF * e : HALF * (e + 1)],
+                lhsT=x_code[g][:, 2 * P * j : 2 * P * (j + 1)].bitcast(FP4X4),
+                lhsT_scale=x_scale[g][:, P * j : P * (j + 1)],
+                rhs=p_code(c, g)[:, 2 * HALF * half : 2 * HALF * (half + 1)].bitcast(FP4X4),
+                rhs_scale=p_scale(c, g)[:, HALF * half : HALF * (half + 1)],
+                start=(g == 0),
+                stop=(g == TP - 1),
+            )
+
+        def first_product(c, b):
+            for e in range(2):
+                for g in range(TP):
+                    first_pass(c, b, e, g)
+
+        def divide(c, b):
+            G, half, u = split(b)
+            if u == 0:
+                pairs[c, G, half] = work.tile([P, 2, PACK, HM, 2], BF16, name="pairs", bufs=3, align_bytes=256)
+            nc.vector.tensor_tensor(
+                out=pairs[c, G, half][:, u, :, :, :],
+                in0=sums[c, b][:].rearrange("p (e m t) -> p t m e", e=2, t=PACK),
+                in1=rmass[c][:, :, HM * half : HM * (half + 1)].unsqueeze(3).to_broadcast([P, PACK, HM, 2]),
+                op=ALU.mult,
+            )
+
+        def group_h(c, G, half):
+            if half == 0:
+                h_group[c, G] = work.tile([P, CHUNK, PACK], BF16, name="h_group", bufs=2, align_bytes=256)
+            words = h_group[c, G][:].rearrange("p n t -> p (n t)").bitcast(F32)
+            nc.scalar.copy(
+                out=words.rearrange("p (t h m u) -> p t h m u", t=PACK, h=2, u=2)[:, :, half, :, :],
+                in_=pairs[c, G, half][:].rearrange("p u t m e -> p (u t m e)").bitcast(F32).rearrange("p (u t m) -> p t m u", u=2, t=PACK),
+            )
+
+        def quantize_h(c, G, parts=1):
+            n = CHUNK // parts
+            for i in range(parts):
+                cols = slice(n * i, n * (i + 1))
+                quantize(h_code[c][G][:, cols], h_scale[c][G][:, cols], h_group[c, G][:, cols, :])
+
+        def second_pass(c, t, G):
+            if G == 0:
+                z_bank[c, t] = bank("z%d_%d" % (c, t))
+            cols = slice(P * t, P * (t + 1))
+            nc.tensor.matmul_mx(
+                out=z_bank[c, t][:],
+                lhsT=h_code[c][G][:, cols].bitcast(FP8X4),
+                lhsT_scale=h_scale[c][G][:, cols],
+                rhs=w_code[G][:].bitcast(FP8X4),
+                rhs_scale=w_scale[G][:],
+                start=(G == 0),
+                stop=(G == FP - 1),
+            )
+
+        def subtract_feat(c, t):
+            nc.gpsimd.tensor_tensor(out=offset[c][t][:], in0=bias_row[:], in1=feat[c][:, t, :], op=ALU.subtract)
+
+        def weigh_offset(c, t):
+            k = PACK * c + t
+            nc.scalar.activation(out=offset[c][t][:], in_=offset[c][t][:], func=ACT.Copy, scale=weight_col[:, k : k + 1])
+
+        def finish(c, t, cols=slice(0, D)):
+            if c not in y_tile:
+                y_tile[c] = work.tile([P, PACK, D], F32, name="y_tile", bufs=2, align_bytes=256)
+                y_group[c] = work.tile([P, D, PACK], BF16, name="y_group", bufs=2, align_bytes=256)
+            k = PACK * c + t
+            nc.vector.scalar_tensor_tensor(
+                out=y_tile[c][:, t, cols],
+                in0=z_bank[c, t][:, cols],
+                scalar=weight_col[:, k : k + 1],
+                in1=offset[c][t][:, cols],
+                op0=ALU.mult,
+                op1=ALU.add,
+            )
+
+        def store_y(c, ts, cols=slice(0, D)):
+            rows = out_0[CHUNK * c : CHUNK * (c + 1), :].rearrange("(p t) d -> p t d", t=PACK)
+            nc.sync.dma_start(out=rows[:, ts, cols], in_=y_tile[c][:, ts, cols])
+
+        def group_y(c, half, engine_copy):
+            cols = slice(HALF * half, HALF * (half + 1))
+            interleave(engine_copy, y_group[c][:, cols, :], y_tile[c][:, :, cols])
+
+        def quantize_y(c, half):
+            cols = slice(HALF * half, HALF * (half + 1))
+            quantize(y_code[c][:, cols], y_scale[c][:, cols], y_group[c][:, cols, :])
+
+        def store_codes(c, cols=slice(0, D)):
+            words = out_1[c].rearrange("p m t -> p (m t)").bitcast(I32)
+            nc.sync.dma_start(out=words[:, cols], in_=y_code[c][:, cols].bitcast(I32))
+
+        def store_scales(c):
+            for q in range(QUADS):
+                nc.sync.dma_start(
+                    out=out_2[c, 4 * q : 4 * q + 4, :].bitcast(I32), in_=y_scale[c][32 * q : 32 * q + 4, :].bitcast(I32)
+                )
+
+        nc.sync.dma_start(out=mass_col[:], in_=mass.rearrange("(c p t) -> p c t", p=P, t=PACK))
+        load_x_words(0)
+        load_p_words(p_first[0], slice(0, 2), 0)
+        nc.vector.memset(xs_raw[:].rearrange("p g n -> p (g n)").bitcast(I32), 0)
+        nc.vector.memset(ps_first[:].rearrange("p g n -> p (g n)").bitcast(I32), 0)
+        make_identity(nc, ident[:])
+        nc.gpsimd.dma_start(out=weight_raw[:], in_=point_weight.rearrange("(c p t) -> p c t", p=P, t=PACK))
+        nc.gpsimd.memset(ps_rest[:].rearrange("p g n -> p (g n)").bitcast(I32), 0)
+        load_scale_rows(xs_raw, x_scales)
+        load_scale_rows(ps_first, p_scales[:, :, 0:CHUNK])
+        load_x_words(1)
+        load_p_words(p_first[1], slice(2, 4), 0)
+        load_x_words(2)
+        load_x_words(3)
+        w_rows = proj_w.rearrange("(q j r) d -> j q r d", j=8, r=8)
+        for j in range(FP * PACK):
+            nc.sync.dma_start(out=w_raw[j // PACK][:, j % PACK, :], in_=w_rows[j])
+        nc.sync.dma_start(out=bias_row[:], in_=bias.partition_broadcast(P))
+        load_feat(0)
+        load_scale_rows(ps_rest, p_scales[:, :, CHUNK:SRC])
+        load_p_words(p_rest[0], slice(0, TP), 1)
+        load_feat(1)
+        load_p_words(p_rest[1], slice(0, TP), 2)
+        load_feat(2)
+
+        nc.vector.reciprocal(out=rmass_col[:], in_=mass_col[:].rearrange("p c t -> p (c t)"))
+        for c in range(NCH):
+            spread = bank("spread%d" % c)
+            for t in range(PACK):
+                k = PACK * c + t
+                nc.tensor.transpose(spread[:, P * t : P * (t + 1)], rmass_col[:, k : k + 1].to_broadcast([P, P]), ident[:])
+            nc.scalar.copy(out=rmass[c][:].rearrange("p t m -> p (t m)"), in_=spread[:])
+        nc.scalar.copy(out=weight_col[:], in_=weight_raw[:].rearrange("p c t -> p (c t)"))
+
+        for c in range(NCH):
+            for t in range(PACK):
+                subtract_feat(c, t)
+
+        for g in range(TP):
+            sort_x_words(g)
+            sort_x_scales(g)
+            for b in range(4):
+                first_pass(0, b, 0, g)
+        group_w(0, 0)
+        group_w(0, 1)
+        group_w(1, 0)
+        for b in range(4):
+            for g in range(TP):
+                first_pass(0, b, 1, g)
+            divide(0, b)
+            if b % 2 == 1:
+                group_h(0, 0, b // 2)
+            if b == 1:
+                quantize_w(0)
+        group_w(1, 1)
+        for b in range(4, 8):
+            first_product(0, b)
+            divide(0, b)
+            if b == 4:
+                quantize_h(0, 0)
+            if b == 5:
+                quantize_w(1)
+            if b % 2 == 1:
+                group_h(0, 1, (b // 2) % 2)
+            if b < 7:
+                weigh_offset(0, b - 4)
+        weigh_offset(0, 3)
+
+        for c in range(1, NCH):
+            lag = 2 if c == 1 else 1
+            quantize_h(c - 1, 1)
+            for b in range(8):
+                first_product(c, b)
+                divide(c, b)
+                if b == 1 and c > 1:
+                    quantize_y(c - 2, 1)
+                    store_codes(c - 2)
+                    store_scales(c - 2)
+                if b % 2 == 1 and b < 7:
+                    group_h(c, b // 4, (b // 2) % 2)
+                if b < 4:
+                    weigh_offset(c, b)
+                t = b - lag
+                if 0 <= t < PACK:
+                    for G in range(FP):
+                        second_pass(c - 1, t, G)
+                    finish(c - 1, t)
+                    if t % 2 == 1:
+                        store_y(c - 1, slice(t - 1, t + 1))
+                if b == 4:
+                    quantize_h(c, 0)
+                if b == 7:
+                    group_h(c, 1, 1)
+                if b == lag + 3:
+                    group_y(c - 1, 0, nc.scalar.copy)
+                if b == 2 * lag + 3:
+                    group_y(c - 1, 1, nc.scalar.copy)
+                if b == lag + 5:
+                    quantize_y(c - 1, 0)
+
+        c = NCH - 1
+        quantize_y(c - 1, 1)
+        store_codes(c - 1)
+        store_scales(c - 1)
+        for t in range(PACK):
+            second_pass(c, t, 0)
+        quantize_h(c, 1, parts=PACK)
+        for t in range(PACK):
+            second_pass(c, t, 1)
+        for half in range(2):
+            cols = slice(HALF * half, HALF * (half + 1))
+            for t in range(PACK):
+                finish(c, t, cols)
+            store_y(c, slice(0, PACK), cols)
+            group_y(c, half, nc.scalar.copy if half == 0 else nc.vector.tensor_copy)
+        for half in range(2):
+            quantize_y(c, half)
+            store_codes(c, slice(HALF * half, HALF * (half + 1)))
+        store_scales(c)

@@ -57,12 +57,14 @@ def tile_drift_mass_residual_k5_kernel(
         w_scale = [kept("w_scale%d" % G, [P, D], U8) for G in range(FP)]
         mass_col = kept("mass_col", [P, NCH, PACK], BF16)
         rmass_col = kept("rmass_col", [P, NCH * PACK], F32)
-        rmass = [kept("rmass%d" % c, [P, PACK, P], F32) for c in range(NCH)]
+        rmass = [kept("rmass%d" % c, [P, CHUNK], F32) for c in range(NCH)]
+        bias_raw = kept("bias_raw", [P, PACK], BF16)
+        bias_col = kept("bias_col", [P, PACK], F32)
         weight_raw = kept("weight_raw", [P, NCH, PACK], BF16)
         weight_col = kept("weight_col", [P, NCH * PACK], F32)
-        bias_row = kept("bias_row", [P, D], BF16)
+        bias_row = kept("bias_row", [P, D], F32)
         feat = [kept("feat%d" % c, [P, PACK, D], BF16) for c in range(NCH)]
-        offset = [[kept("offset%d_%d" % (c, t), [P, D], F32) for t in range(PACK)] for c in range(NCH)]
+        offset = [kept("offset%d" % t, [P, D], F32) for t in range(PACK)]
         h_code = [[kept("h_code%d_%d" % (c, G), [P, CHUNK], U32) for G in range(FP)] for c in range(NCH)]
         h_scale = [[kept("h_scale%d_%d" % (c, G), [P, CHUNK], U8) for G in range(FP)] for c in range(NCH)]
         y_code = [kept("y_code%d" % c, [P, D], U32) for c in range(NCH)]
@@ -114,9 +116,9 @@ def tile_drift_mass_residual_k5_kernel(
         def quantize(codes, scales, grouped):
             nc.vector.quantize_mx(out=codes.bitcast(FP8X4), scales=scales, in_=grouped.rearrange("p n t -> p (n t)"))
 
-        def group_w(G, half):
+        def group_w(G, half, engine_copy):
             cols = slice(HALF * half, HALF * (half + 1))
-            interleave(nc.scalar.copy, w_group[G][:, cols, :], w_raw[G][:, :, cols])
+            interleave(engine_copy, w_group[G][:, cols, :], w_raw[G][:, :, cols])
 
         def quantize_w(G):
             quantize(w_code[G][:], w_scale[G][:], w_group[G][:])
@@ -154,11 +156,11 @@ def tile_drift_mass_residual_k5_kernel(
         def divide(c, b):
             G, half, u = split(b)
             if u == 0:
-                pairs[c, G, half] = work.tile([P, 2, PACK, HM, 2], BF16, name="pairs", bufs=3, align_bytes=256)
+                pairs[c, G, half] = work.tile([P, 2, HALF, 2], BF16, name="pairs", bufs=3, align_bytes=256)
             nc.vector.tensor_tensor(
-                out=pairs[c, G, half][:, u, :, :, :],
-                in0=sums[c, b][:].rearrange("p (e m t) -> p t m e", e=2, t=PACK),
-                in1=rmass[c][:, :, HM * half : HM * (half + 1)].unsqueeze(3).to_broadcast([P, PACK, HM, 2]),
+                out=pairs[c, G, half][:, u, :, :],
+                in0=sums[c, b][:].rearrange("p (e s) -> p s e", e=2),
+                in1=rmass[c][:, HALF * half : HALF * (half + 1)].unsqueeze(2).to_broadcast([P, HALF, 2]),
                 op=ALU.mult,
             )
 
@@ -167,8 +169,8 @@ def tile_drift_mass_residual_k5_kernel(
                 h_group[c, G] = work.tile([P, CHUNK, PACK], BF16, name="h_group", bufs=2, align_bytes=256)
             words = h_group[c, G][:].rearrange("p n t -> p (n t)").bitcast(F32)
             nc.scalar.copy(
-                out=words.rearrange("p (t h m u) -> p t h m u", t=PACK, h=2, u=2)[:, :, half, :, :],
-                in_=pairs[c, G, half][:].rearrange("p u t m e -> p (u t m e)").bitcast(F32).rearrange("p (u t m) -> p t m u", u=2, t=PACK),
+                out=words.rearrange("p (t h m u) -> p h m t u", t=PACK, h=2, u=2)[:, half, :, :, :],
+                in_=pairs[c, G, half][:].rearrange("p u s e -> p (u s e)").bitcast(F32).rearrange("p (u m t) -> p m t u", u=2, t=PACK),
             )
 
         def quantize_h(c, G, parts=1):
@@ -192,11 +194,11 @@ def tile_drift_mass_residual_k5_kernel(
             )
 
         def subtract_feat(c, t):
-            nc.gpsimd.tensor_tensor(out=offset[c][t][:], in0=bias_row[:], in1=feat[c][:, t, :], op=ALU.subtract)
+            nc.gpsimd.tensor_tensor(out=offset[t][:], in0=bias_row[:], in1=feat[c][:, t, :], op=ALU.subtract)
 
         def weigh_offset(c, t):
             k = PACK * c + t
-            nc.scalar.activation(out=offset[c][t][:], in_=offset[c][t][:], func=ACT.Copy, scale=weight_col[:, k : k + 1])
+            nc.scalar.activation(out=offset[t][:], in_=offset[t][:], func=ACT.Copy, scale=weight_col[:, k : k + 1])
 
         def finish(c, t, cols=slice(0, D)):
             if c not in y_tile:
@@ -207,7 +209,7 @@ def tile_drift_mass_residual_k5_kernel(
                 out=y_tile[c][:, t, cols],
                 in0=z_bank[c, t][:, cols],
                 scalar=weight_col[:, k : k + 1],
-                in1=offset[c][t][:, cols],
+                in1=offset[t][:, cols],
                 op0=ALU.mult,
                 op1=ALU.add,
             )
@@ -228,20 +230,29 @@ def tile_drift_mass_residual_k5_kernel(
             words = out_1[c].rearrange("p m t -> p (m t)").bitcast(I32)
             nc.sync.dma_start(out=words[:, cols], in_=y_code[c][:, cols].bitcast(I32))
 
-        def store_scales(c):
+        def store_scales(c, queues=(nc.sync, nc.sync)):
             for q in range(QUADS):
-                nc.sync.dma_start(
+                queues[q % 2].dma_start(
                     out=out_2[c, 4 * q : 4 * q + 4, :].bitcast(I32), in_=y_scale[c][32 * q : 32 * q + 4, :].bitcast(I32)
                 )
 
+        def spread(name, dst, columns):
+            rows = bank(name)
+            for t in range(PACK):
+                nc.tensor.transpose(rows[:, P * t : P * (t + 1)], columns[:, t : t + 1].to_broadcast([P, P]), ident[:])
+            nc.scalar.copy(out=dst.rearrange("p (m t) -> p m t", t=PACK), in_=rows[:].rearrange("p (t m) -> p m t", t=PACK))
+
         nc.sync.dma_start(out=mass_col[:], in_=mass.rearrange("(c p t) -> p c t", p=P, t=PACK))
+        nc.sync.dma_start(out=bias_raw[:], in_=bias.rearrange("(p t) -> p t", t=PACK))
         load_x_words(0)
         load_p_words(p_first[0], slice(0, 2), 0)
         nc.vector.memset(xs_raw[:].rearrange("p g n -> p (g n)").bitcast(I32), 0)
         nc.vector.memset(ps_first[:].rearrange("p g n -> p (g n)").bitcast(I32), 0)
+        nc.vector.reciprocal(out=rmass_col[:], in_=mass_col[:].rearrange("p c t -> p (c t)"))
+        nc.vector.tensor_copy(out=bias_col[:], in_=bias_raw[:])
+        nc.vector.memset(ps_rest[:].rearrange("p g n -> p (g n)").bitcast(I32), 0)
         make_identity(nc, ident[:])
         nc.gpsimd.dma_start(out=weight_raw[:], in_=point_weight.rearrange("(c p t) -> p c t", p=P, t=PACK))
-        nc.gpsimd.memset(ps_rest[:].rearrange("p g n -> p (g n)").bitcast(I32), 0)
         load_scale_rows(xs_raw, x_scales)
         load_scale_rows(ps_first, p_scales[:, :, 0:CHUNK])
         load_x_words(1)
@@ -251,7 +262,6 @@ def tile_drift_mass_residual_k5_kernel(
         w_rows = proj_w.rearrange("(q j r) d -> j q r d", j=8, r=8)
         for j in range(FP * PACK):
             nc.sync.dma_start(out=w_raw[j // PACK][:, j % PACK, :], in_=w_rows[j])
-        nc.sync.dma_start(out=bias_row[:], in_=bias.partition_broadcast(P))
         load_feat(0)
         load_scale_rows(ps_rest, p_scales[:, :, CHUNK:SRC])
         load_p_words(p_rest[0], slice(0, TP), 1)
@@ -259,48 +269,38 @@ def tile_drift_mass_residual_k5_kernel(
         load_p_words(p_rest[1], slice(0, TP), 2)
         load_feat(2)
 
-        nc.vector.reciprocal(out=rmass_col[:], in_=mass_col[:].rearrange("p c t -> p (c t)"))
+        nc.scalar.activation(out=weight_col[:], in_=weight_raw[:].rearrange("p c t -> p (c t)"), func=ACT.Copy)
         for c in range(NCH):
-            spread = bank("spread%d" % c)
-            for t in range(PACK):
-                k = PACK * c + t
-                nc.tensor.transpose(spread[:, P * t : P * (t + 1)], rmass_col[:, k : k + 1].to_broadcast([P, P]), ident[:])
-            nc.scalar.copy(out=rmass[c][:].rearrange("p t m -> p (t m)"), in_=spread[:])
-        nc.scalar.copy(out=weight_col[:], in_=weight_raw[:].rearrange("p c t -> p (c t)"))
+            spread("rmass_rows%d" % c, rmass[c][:], rmass_col[:, PACK * c : PACK * (c + 1)])
+        spread("bias_rows", bias_row[:], bias_col[:])
 
-        for c in range(NCH):
-            for t in range(PACK):
-                subtract_feat(c, t)
-
+        for t in range(PACK):
+            subtract_feat(0, t)
         for g in range(TP):
             sort_x_words(g)
             sort_x_scales(g)
             for b in range(4):
                 first_pass(0, b, 0, g)
-        group_w(0, 0)
-        group_w(0, 1)
-        group_w(1, 0)
+        for half in range(2):
+            group_w(0, half, nc.vector.tensor_copy)
+            group_w(1, half, nc.scalar.copy)
+        quantize_w(0)
         for b in range(4):
             for g in range(TP):
                 first_pass(0, b, 1, g)
             divide(0, b)
             if b % 2 == 1:
                 group_h(0, 0, b // 2)
-            if b == 1:
-                quantize_w(0)
-        group_w(1, 1)
         for b in range(4, 8):
             first_product(0, b)
             divide(0, b)
-            if b == 4:
-                quantize_h(0, 0)
-            if b == 5:
-                quantize_w(1)
             if b % 2 == 1:
                 group_h(0, 1, (b // 2) % 2)
-            if b < 7:
-                weigh_offset(0, b - 4)
-        weigh_offset(0, 3)
+            weigh_offset(0, b - 4)
+            if b == 6:
+                quantize_h(0, 0)
+            if b == 7:
+                quantize_w(1)
 
         for c in range(1, NCH):
             lag = 2 if c == 1 else 1
@@ -308,39 +308,37 @@ def tile_drift_mass_residual_k5_kernel(
             for b in range(8):
                 first_product(c, b)
                 divide(c, b)
-                if b == 1 and c > 1:
-                    quantize_y(c - 2, 1)
-                    store_codes(c - 2)
-                    store_scales(c - 2)
-                if b % 2 == 1 and b < 7:
+                if b % 2 == 1:
                     group_h(c, b // 4, (b // 2) % 2)
-                if b < 4:
-                    weigh_offset(c, b)
                 t = b - lag
+                if 1 <= t <= PACK:
+                    weigh_offset(c, t - 1)
                 if 0 <= t < PACK:
                     for G in range(FP):
                         second_pass(c - 1, t, G)
                     finish(c - 1, t)
+                    subtract_feat(c, t)
                     if t % 2 == 1:
                         store_y(c - 1, slice(t - 1, t + 1))
+                if b == 1 and c > 1:
+                    quantize_y(c - 2, 1)
+                    store_codes(c - 2)
+                    store_scales(c - 2)
                 if b == 4:
                     quantize_h(c, 0)
-                if b == 7:
-                    group_h(c, 1, 1)
-                if b == lag + 3:
+                if t == 3:
                     group_y(c - 1, 0, nc.scalar.copy)
-                if b == 2 * lag + 3:
+                if t == 5:
                     group_y(c - 1, 1, nc.scalar.copy)
-                if b == lag + 5:
                     quantize_y(c - 1, 0)
 
         c = NCH - 1
-        quantize_y(c - 1, 1)
-        store_codes(c - 1)
-        store_scales(c - 1)
         for t in range(PACK):
             second_pass(c, t, 0)
         quantize_h(c, 1, parts=PACK)
+        quantize_y(c - 1, 1)
+        store_codes(c - 1)
+        store_scales(c - 1)
         for t in range(PACK):
             second_pass(c, t, 1)
         for half in range(2):
@@ -352,4 +350,4 @@ def tile_drift_mass_residual_k5_kernel(
         for half in range(2):
             quantize_y(c, half)
             store_codes(c, slice(HALF * half, HALF * (half + 1)))
-        store_scales(c)
+        store_scales(c, (nc.sync, nc.scalar))

@@ -47,7 +47,8 @@ def tile_drift_mass_residual_k5_kernel(
         x_code = [kept("x_code%d" % g, [P, 2 * F], U8) for g in range(TP)]
         xs_raw = kept("xs_raw", [P, TP, F], U8)
         x_scale = [kept("x_scale%d" % g, [P, F], U8) for g in range(TP)]
-        p_first = [kept("p_first%d" % i, [P, 2, 2 * CHUNK], U8) for i in range(2)]
+        first_loads = [slice(0, 1), slice(1, 2), slice(2, TP)]
+        p_first = [kept("p_first%d" % gs.start, [P, gs.stop - gs.start, 2 * CHUNK], U8) for gs in first_loads]
         p_rest = [kept("p_rest%d" % c, [P, TP, 2 * CHUNK], U8) for c in range(NCH - 1)]
         ps_first = kept("ps_first", [P, TP, CHUNK], U8)
         ps_rest = kept("ps_rest", [P, TP, SRC - CHUNK], U8)
@@ -55,14 +56,13 @@ def tile_drift_mass_residual_k5_kernel(
         w_group = [kept("w_group%d" % G, [P, D, PACK], BF16) for G in range(FP)]
         w_code = [kept("w_code%d" % G, [P, D], U32) for G in range(FP)]
         w_scale = [kept("w_scale%d" % G, [P, D], U8) for G in range(FP)]
-        mass_col = kept("mass_col", [P, NCH, PACK], BF16)
+        mass_col = kept("mass_col", [P, NCH * PACK], BF16)
         rmass_col = kept("rmass_col", [P, NCH * PACK], F32)
-        rmass = [kept("rmass%d" % c, [P, CHUNK], F32) for c in range(NCH)]
+        rmass = kept("rmass", [P, SRC], F32)
         bias_raw = kept("bias_raw", [P, PACK], BF16)
-        bias_col = kept("bias_col", [P, PACK], F32)
         weight_raw = kept("weight_raw", [P, NCH, PACK], BF16)
         weight_col = kept("weight_col", [P, NCH * PACK], F32)
-        bias_row = kept("bias_row", [P, D], F32)
+        bias_row = kept("bias_row", [P, D], BF16)
         feat = [kept("feat%d" % c, [P, PACK, D], BF16) for c in range(NCH)]
         offset = [kept("offset%d" % t, [P, D], F32) for t in range(PACK)]
         h_code = [[kept("h_code%d_%d" % (c, G), [P, CHUNK], U32) for G in range(FP)] for c in range(NCH)]
@@ -72,7 +72,7 @@ def tile_drift_mass_residual_k5_kernel(
         ident = kept("ident", [P, P], F32)
 
         def p_code(c, g):
-            return p_first[g // 2][:, g % 2, :] if c == 0 else p_rest[c - 1][:, g, :]
+            return p_first[min(g, 2)][:, g - min(g, 2), :] if c == 0 else p_rest[c - 1][:, g, :]
 
         def p_scale(c, g):
             return ps_first[:, g, :] if c == 0 else ps_rest[:, g, (c - 1) * CHUNK : c * CHUNK]
@@ -153,24 +153,26 @@ def tile_drift_mass_residual_k5_kernel(
                 for g in range(TP):
                     first_pass(c, b, e, g)
 
-        def divide(c, b):
+        def divide(c, b, part=slice(0, HALF)):
             G, half, u = split(b)
-            if u == 0:
+            s0 = CHUNK * c + HALF * half
+            n = part.stop - part.start
+            if (c, G, half) not in pairs:
                 pairs[c, G, half] = work.tile([P, 2, HALF, 2], BF16, name="pairs", bufs=3, align_bytes=256)
             nc.vector.tensor_tensor(
-                out=pairs[c, G, half][:, u, :, :],
-                in0=sums[c, b][:].rearrange("p (e s) -> p s e", e=2),
-                in1=rmass[c][:, HALF * half : HALF * (half + 1)].unsqueeze(2).to_broadcast([P, HALF, 2]),
+                out=pairs[c, G, half][:, u, part, :],
+                in0=sums[c, b][:].rearrange("p (e s) -> p s e", e=2)[:, part, :],
+                in1=rmass[:, s0 + part.start : s0 + part.stop].unsqueeze(2).to_broadcast([P, n, 2]),
                 op=ALU.mult,
             )
 
-        def group_h(c, G, half):
+        def group_h(c, G, half, ms=slice(0, HM)):
             if half == 0:
                 h_group[c, G] = work.tile([P, CHUNK, PACK], BF16, name="h_group", bufs=2, align_bytes=256)
             words = h_group[c, G][:].rearrange("p n t -> p (n t)").bitcast(F32)
             nc.scalar.copy(
-                out=words.rearrange("p (t h m u) -> p h m t u", t=PACK, h=2, u=2)[:, half, :, :, :],
-                in_=pairs[c, G, half][:].rearrange("p u s e -> p (u s e)").bitcast(F32).rearrange("p (u m t) -> p m t u", u=2, t=PACK),
+                out=words.rearrange("p (t h m u) -> p h m t u", t=PACK, h=2, u=2)[:, half, ms, :, :],
+                in_=pairs[c, G, half][:].rearrange("p u s e -> p (u s e)").bitcast(F32).rearrange("p (u m t) -> p m t u", u=2, t=PACK)[:, ms, :, :],
             )
 
         def quantize_h(c, G, parts=1):
@@ -179,22 +181,23 @@ def tile_drift_mass_residual_k5_kernel(
                 cols = slice(n * i, n * (i + 1))
                 quantize(h_code[c][G][:, cols], h_scale[c][G][:, cols], h_group[c, G][:, cols, :])
 
-        def second_pass(c, t, G):
+        def second_pass(c, t, G, ds=slice(0, D)):
             if G == 0:
-                z_bank[c, t] = bank("z%d_%d" % (c, t))
+                z_bank[c, t, ds.start // HALF] = bank("z%d_%d_%d" % (c, t, ds.start))
+                z_bank[c, t, (ds.stop - 1) // HALF] = z_bank[c, t, ds.start // HALF]
             cols = slice(P * t, P * (t + 1))
             nc.tensor.matmul_mx(
-                out=z_bank[c, t][:],
+                out=z_bank[c, t, ds.start // HALF][:, ds],
                 lhsT=h_code[c][G][:, cols].bitcast(FP8X4),
                 lhsT_scale=h_scale[c][G][:, cols],
-                rhs=w_code[G][:].bitcast(FP8X4),
-                rhs_scale=w_scale[G][:],
+                rhs=w_code[G][:, ds].bitcast(FP8X4),
+                rhs_scale=w_scale[G][:, ds],
                 start=(G == 0),
                 stop=(G == FP - 1),
             )
 
-        def subtract_feat(c, t):
-            nc.gpsimd.tensor_tensor(out=offset[t][:], in0=bias_row[:], in1=feat[c][:, t, :], op=ALU.subtract)
+        def subtract_feat(c, t, cols=slice(0, D)):
+            nc.gpsimd.tensor_tensor(out=offset[t][:, cols], in0=bias_row[:, cols], in1=feat[c][:, t, cols], op=ALU.subtract)
 
         def weigh_offset(c, t):
             k = PACK * c + t
@@ -207,7 +210,7 @@ def tile_drift_mass_residual_k5_kernel(
             k = PACK * c + t
             nc.vector.scalar_tensor_tensor(
                 out=y_tile[c][:, t, cols],
-                in0=z_bank[c, t][:, cols],
+                in0=z_bank[c, t, cols.start // HALF][:, cols],
                 scalar=weight_col[:, k : k + 1],
                 in1=offset[t][:, cols],
                 op0=ALU.mult,
@@ -218,12 +221,10 @@ def tile_drift_mass_residual_k5_kernel(
             rows = out_0[CHUNK * c : CHUNK * (c + 1), :].rearrange("(p t) d -> p t d", t=PACK)
             nc.sync.dma_start(out=rows[:, ts, cols], in_=y_tile[c][:, ts, cols])
 
-        def group_y(c, half, engine_copy):
-            cols = slice(HALF * half, HALF * (half + 1))
-            interleave(engine_copy, y_group[c][:, cols, :], y_tile[c][:, :, cols])
+        def group_y(c, cols):
+            interleave(nc.scalar.copy, y_group[c][:, cols, :], y_tile[c][:, :, cols])
 
-        def quantize_y(c, half):
-            cols = slice(HALF * half, HALF * (half + 1))
+        def quantize_y(c, cols):
             quantize(y_code[c][:, cols], y_scale[c][:, cols], y_group[c][:, cols, :])
 
         def store_codes(c, cols=slice(0, D)):
@@ -238,26 +239,30 @@ def tile_drift_mass_residual_k5_kernel(
 
         def spread(name, dst, columns):
             rows = bank(name)
-            for t in range(PACK):
+            n = columns.shape[1]
+            for t in range(n):
                 nc.tensor.transpose(rows[:, P * t : P * (t + 1)], columns[:, t : t + 1].to_broadcast([P, P]), ident[:])
-            nc.scalar.copy(out=dst.rearrange("p (m t) -> p m t", t=PACK), in_=rows[:].rearrange("p (t m) -> p m t", t=PACK))
+            nc.scalar.copy(out=dst, in_=rows[:, 0 : P * n].rearrange("p (t m) -> p m t", t=n))
 
-        nc.sync.dma_start(out=mass_col[:], in_=mass.rearrange("(c p t) -> p c t", p=P, t=PACK))
+        halves = [slice(0, HALF), slice(HALF, D)]
+        quarters = [slice(P * i, P * (i + 1)) for i in range(4)]
+
+        nc.sync.dma_start(out=mass_col[:], in_=mass.rearrange("(p j) -> p j", p=P))
         nc.sync.dma_start(out=bias_raw[:], in_=bias.rearrange("(p t) -> p t", t=PACK))
         load_x_words(0)
-        load_p_words(p_first[0], slice(0, 2), 0)
+        load_p_words(p_first[0], first_loads[0], 0)
         nc.vector.memset(xs_raw[:].rearrange("p g n -> p (g n)").bitcast(I32), 0)
         nc.vector.memset(ps_first[:].rearrange("p g n -> p (g n)").bitcast(I32), 0)
-        nc.vector.reciprocal(out=rmass_col[:], in_=mass_col[:].rearrange("p c t -> p (c t)"))
-        nc.vector.tensor_copy(out=bias_col[:], in_=bias_raw[:])
+        nc.vector.reciprocal(out=rmass_col[:], in_=mass_col[:])
         nc.vector.memset(ps_rest[:].rearrange("p g n -> p (g n)").bitcast(I32), 0)
         make_identity(nc, ident[:])
         nc.gpsimd.dma_start(out=weight_raw[:], in_=point_weight.rearrange("(c p t) -> p c t", p=P, t=PACK))
         load_scale_rows(xs_raw, x_scales)
         load_scale_rows(ps_first, p_scales[:, :, 0:CHUNK])
         load_x_words(1)
-        load_p_words(p_first[1], slice(2, 4), 0)
+        load_p_words(p_first[1], first_loads[1], 0)
         load_x_words(2)
+        load_p_words(p_first[2], first_loads[2], 0)
         load_x_words(3)
         w_rows = proj_w.rearrange("(q j r) d -> j q r d", j=8, r=8)
         for j in range(FP * PACK):
@@ -269,49 +274,58 @@ def tile_drift_mass_residual_k5_kernel(
         load_p_words(p_rest[1], slice(0, TP), 2)
         load_feat(2)
 
+        rmass_runs = rmass[:].rearrange("p (m j) -> p m j", m=P)
+        for i in range(NCH):
+            js = slice(PACK * i, PACK * (i + 1))
+            spread("rmass_rows%d" % i, rmass_runs[:, :, js], rmass_col[:, js])
+        spread("bias_rows", bias_row[:].bitcast(F32).rearrange("p (m u) -> p m u", u=2), bias_raw[:].bitcast(F32))
         nc.scalar.activation(out=weight_col[:], in_=weight_raw[:].rearrange("p c t -> p (c t)"), func=ACT.Copy)
-        for c in range(NCH):
-            spread("rmass_rows%d" % c, rmass[c][:], rmass_col[:, PACK * c : PACK * (c + 1)])
-        spread("bias_rows", bias_row[:], bias_col[:])
 
+        early = 6
         for t in range(PACK):
-            subtract_feat(0, t)
+            for cols in halves:
+                subtract_feat(0, t, cols)
         for g in range(TP):
             sort_x_words(g)
             sort_x_scales(g)
-            for b in range(4):
+            for b in range(early):
                 first_pass(0, b, 0, g)
         for half in range(2):
             group_w(0, half, nc.vector.tensor_copy)
             group_w(1, half, nc.scalar.copy)
         quantize_w(0)
-        for b in range(4):
-            for g in range(TP):
-                first_pass(0, b, 1, g)
+        for b in range(8):
+            if b < early:
+                for g in range(TP):
+                    first_pass(0, b, 1, g)
+            else:
+                first_product(0, b)
             divide(0, b)
             if b % 2 == 1:
-                group_h(0, 0, b // 2)
-        for b in range(4, 8):
-            first_product(0, b)
-            divide(0, b)
-            if b % 2 == 1:
-                group_h(0, 1, (b // 2) % 2)
-            weigh_offset(0, b - 4)
-            if b == 6:
+                group_h(0, b // 4, (b // 2) % 2)
+            if b >= 4:
+                weigh_offset(0, b - 4)
+            if b == 5:
                 quantize_h(0, 0)
-            if b == 7:
+            if b == 6:
                 quantize_w(1)
 
         for c in range(1, NCH):
-            lag = 2 if c == 1 else 1
+            last = c == NCH - 1
+            lag = 1 if last else 2
             quantize_h(c - 1, 1)
             for b in range(8):
                 first_product(c, b)
-                divide(c, b)
-                if b % 2 == 1:
-                    group_h(c, b // 4, (b // 2) % 2)
+                if last and b == 7:
+                    for i in range(2):
+                        divide(c, b, quarters[i])
+                        group_h(c, 1, 1, slice(32 * i, 32 * (i + 1)))
+                else:
+                    divide(c, b)
+                    if b % 2 == 1:
+                        group_h(c, b // 4, (b // 2) % 2)
                 t = b - lag
-                if 1 <= t <= PACK:
+                if 1 <= t <= PACK - last:
                     weigh_offset(c, t - 1)
                 if 0 <= t < PACK:
                     for G in range(FP):
@@ -321,33 +335,39 @@ def tile_drift_mass_residual_k5_kernel(
                     if t % 2 == 1:
                         store_y(c - 1, slice(t - 1, t + 1))
                 if b == 1 and c > 1:
-                    quantize_y(c - 2, 1)
+                    quantize_y(c - 2, halves[1])
                     store_codes(c - 2)
                     store_scales(c - 2)
                 if b == 4:
                     quantize_h(c, 0)
                 if t == 3:
-                    group_y(c - 1, 0, nc.scalar.copy)
+                    group_y(c - 1, halves[0])
+                if b == (5 if last else 7):
+                    group_y(c - 1, halves[1])
                 if t == 5:
-                    group_y(c - 1, 1, nc.scalar.copy)
-                    quantize_y(c - 1, 0)
+                    quantize_y(c - 1, halves[0])
 
         c = NCH - 1
-        for t in range(PACK):
-            second_pass(c, t, 0)
-        quantize_h(c, 1, parts=PACK)
-        quantize_y(c - 1, 1)
+        weigh_offset(c, PACK - 1)
+        quantize_y(c - 1, halves[1])
         store_codes(c - 1)
         store_scales(c - 1)
-        for t in range(PACK):
-            second_pass(c, t, 1)
-        for half in range(2):
-            cols = slice(HALF * half, HALF * (half + 1))
+        for ds in halves:
+            for t in range(PACK):
+                second_pass(c, t, 0, ds)
+        quantize_h(c, 1, parts=PACK)
+        for ds in halves:
+            for t in range(PACK):
+                second_pass(c, t, 1, ds)
+        for i, cols in enumerate(quarters):
             for t in range(PACK):
                 finish(c, t, cols)
-            store_y(c, slice(0, PACK), cols)
-            group_y(c, half, nc.scalar.copy if half == 0 else nc.vector.tensor_copy)
-        for half in range(2):
-            quantize_y(c, half)
-            store_codes(c, slice(HALF * half, HALF * (half + 1)))
+            group_y(c, cols)
+            if i % 2 == 1:
+                store_y(c, slice(0, PACK), halves[i // 2])
+        quantize_y(c, halves[0])
+        store_codes(c, halves[0])
+        quantize_y(c, quarters[2])
+        quantize_y(c, quarters[3])
+        store_codes(c, halves[1])
         store_scales(c, (nc.sync, nc.scalar))

@@ -45,7 +45,7 @@ def tile_drift_mass_residual_k5_kernel(
 
         x_raw = [kept("x_raw%d" % g, [P, 2 * F], U8) for g in range(TP)]
         x_code = [kept("x_code%d" % g, [P, 2 * F], U8) for g in range(TP)]
-        xs_raw = kept("xs_raw", [P, TP, F], U8)
+        xs_raw = [kept("xs_raw%d" % i, [P, 2, F], U8) for i in range(2)]
         x_scale = [kept("x_scale%d" % g, [P, F], U8) for g in range(TP)]
         first_loads = [slice(0, 1), slice(1, 2), slice(2, TP)]
         p_first = [kept("p_first%d" % gs.start, [P, gs.stop - gs.start, 2 * CHUNK], U8) for gs in first_loads]
@@ -104,7 +104,7 @@ def tile_drift_mass_residual_k5_kernel(
         def sort_x_scales(g):
             nc.vector.tensor_copy(
                 out=x_scale[g][:].bitcast(I32).rearrange("p (j q w) -> p j q w", j=8, w=2),
-                in_=xs_raw[:, g, :].bitcast(I32).rearrange("p (q j w) -> p j q w", j=8, w=2),
+                in_=xs_raw[g // 2][:, g % 2, :].bitcast(I32).rearrange("p (q j w) -> p j q w", j=8, w=2),
             )
 
         def interleave(engine_copy, dst, src):
@@ -221,8 +221,8 @@ def tile_drift_mass_residual_k5_kernel(
             rows = out_0[CHUNK * c : CHUNK * (c + 1), :].rearrange("(p t) d -> p t d", t=PACK)
             nc.sync.dma_start(out=rows[:, ts, cols], in_=y_tile[c][:, ts, cols])
 
-        def group_y(c, cols):
-            interleave(nc.scalar.copy, y_group[c][:, cols, :], y_tile[c][:, :, cols])
+        def group_y(c, cols, engine_copy=nc.scalar.copy):
+            interleave(engine_copy, y_group[c][:, cols, :], y_tile[c][:, :, cols])
 
         def quantize_y(c, cols):
             quantize(y_code[c][:, cols], y_scale[c][:, cols], y_group[c][:, cols, :])
@@ -251,23 +251,26 @@ def tile_drift_mass_residual_k5_kernel(
         nc.sync.dma_start(out=bias_raw[:], in_=bias.rearrange("(p t) -> p t", t=PACK))
         load_x_words(0)
         load_p_words(p_first[0], first_loads[0], 0)
-        nc.vector.memset(xs_raw[:].rearrange("p g n -> p (g n)").bitcast(I32), 0)
+        nc.vector.memset(xs_raw[0][:].rearrange("p g n -> p (g n)").bitcast(I32), 0)
         nc.vector.memset(ps_first[:].rearrange("p g n -> p (g n)").bitcast(I32), 0)
+        nc.vector.memset(xs_raw[1][:].rearrange("p g n -> p (g n)").bitcast(I32), 0)
         nc.vector.reciprocal(out=rmass_col[:], in_=mass_col[:])
         nc.vector.memset(ps_rest[:].rearrange("p g n -> p (g n)").bitcast(I32), 0)
         make_identity(nc, ident[:])
         nc.gpsimd.dma_start(out=weight_raw[:], in_=point_weight.rearrange("(c p t) -> p c t", p=P, t=PACK))
-        load_scale_rows(xs_raw, x_scales)
+        load_scale_rows(xs_raw[0], x_scales[0:2])
         load_scale_rows(ps_first, p_scales[:, :, 0:CHUNK])
         load_x_words(1)
         load_p_words(p_first[1], first_loads[1], 0)
+        load_scale_rows(xs_raw[1], x_scales[2:4])
         load_x_words(2)
         load_p_words(p_first[2], first_loads[2], 0)
         load_x_words(3)
         w_rows = proj_w.rearrange("(q j r) d -> j q r d", j=8, r=8)
         for j in range(FP * PACK):
             nc.sync.dma_start(out=w_raw[j // PACK][:, j % PACK, :], in_=w_rows[j])
-        load_feat(0)
+            if j == PACK - 1:
+                load_feat(0)
         load_scale_rows(ps_rest, p_scales[:, :, CHUNK:SRC])
         load_p_words(p_rest[0], slice(0, TP), 1)
         load_feat(1)
@@ -292,7 +295,6 @@ def tile_drift_mass_residual_k5_kernel(
                 first_pass(0, b, 0, g)
         for half in range(2):
             group_w(0, half, nc.vector.tensor_copy)
-            group_w(1, half, nc.scalar.copy)
         quantize_w(0)
         for b in range(8):
             if b < early:
@@ -303,53 +305,77 @@ def tile_drift_mass_residual_k5_kernel(
             divide(0, b)
             if b % 2 == 1:
                 group_h(0, b // 4, (b // 2) % 2)
-            if b >= 4:
-                weigh_offset(0, b - 4)
-            if b == 5:
-                quantize_h(0, 0)
-            if b == 6:
-                quantize_w(1)
+            if b in (3, 5):
+                group_w(1, (b - 3) // 2, nc.scalar.copy)
+        quantize_h(0, 0)
+        quantize_w(1)
+        quantize_h(0, 1)
 
-        for c in range(1, NCH):
-            last = c == NCH - 1
-            lag = 1 if last else 2
-            quantize_h(c - 1, 1)
-            for b in range(8):
-                first_product(c, b)
-                if last and b == 7:
-                    for i in range(2):
-                        divide(c, b, quarters[i])
-                        group_h(c, 1, 1, slice(32 * i, 32 * (i + 1)))
-                else:
-                    divide(c, b)
-                    if b % 2 == 1:
-                        group_h(c, b // 4, (b // 2) % 2)
-                t = b - lag
-                if 1 <= t <= PACK - last:
-                    weigh_offset(c, t - 1)
-                if 0 <= t < PACK:
-                    for G in range(FP):
-                        second_pass(c - 1, t, G)
-                    finish(c - 1, t)
-                    subtract_feat(c, t)
-                    if t % 2 == 1:
-                        store_y(c - 1, slice(t - 1, t + 1))
-                if b == 1 and c > 1:
-                    quantize_y(c - 2, halves[1])
-                    store_codes(c - 2)
-                    store_scales(c - 2)
-                if b == 4:
-                    quantize_h(c, 0)
-                if t == 3:
-                    group_y(c - 1, halves[0])
-                if b == (5 if last else 7):
-                    group_y(c - 1, halves[1])
-                if t == 5:
-                    quantize_y(c - 1, halves[0])
+        for b in range(8):
+            first_product(1, b)
+            divide(1, b)
+            if b < 2:
+                weigh_offset(0, 2 * b)
+            if b % 2 == 1:
+                group_h(1, b // 4, (b // 2) % 2)
+            if b < 2:
+                weigh_offset(0, 2 * b + 1)
+            t = b - 2
+            if t in (1, 2):
+                weigh_offset(1, t - 1)
+            if 0 <= t < PACK:
+                for G in range(FP):
+                    second_pass(0, t, G)
+                finish(0, t)
+                subtract_feat(1, t)
+                if t % 2 == 1:
+                    store_y(0, slice(t - 1, t + 1))
+            if b == 4:
+                quantize_h(1, 0)
+            if b == 5:
+                group_y(0, halves[0])
+                weigh_offset(1, 2)
+        quantize_y(0, halves[0])
+        weigh_offset(1, 3)
+        group_y(0, halves[1])
+        quantize_h(1, 1)
+
+        for b in range(8):
+            first_product(2, b)
+            if b == 7:
+                for i in range(2):
+                    divide(2, b, quarters[i])
+                    group_h(2, 1, 1, slice(32 * i, 32 * (i + 1)))
+            else:
+                divide(2, b)
+                if b % 2 == 1:
+                    group_h(2, b // 4, (b // 2) % 2)
+            t = b - 1
+            if t in (1, 2):
+                weigh_offset(2, t - 1)
+            if 0 <= t < PACK:
+                for G in range(FP):
+                    second_pass(1, t, G)
+                finish(1, t)
+                subtract_feat(2, t)
+                if t % 2 == 1:
+                    store_y(1, slice(t - 1, t + 1))
+            if b == 2:
+                quantize_y(0, halves[1])
+                store_codes(0)
+                store_scales(0)
+            if b == 4:
+                quantize_h(2, 0)
+                group_y(1, halves[0])
+            if b == 5:
+                group_y(1, quarters[2])
+            if b == 6:
+                group_y(1, quarters[3], nc.vector.tensor_copy)
 
         c = NCH - 1
-        weigh_offset(c, PACK - 1)
-        quantize_y(c - 1, halves[1])
+        weigh_offset(c, 2)
+        weigh_offset(c, 3)
+        quantize_y(c - 1, slice(0, D))
         store_codes(c - 1)
         store_scales(c - 1)
         for ds in halves:
@@ -362,11 +388,13 @@ def tile_drift_mass_residual_k5_kernel(
         for i, cols in enumerate(quarters):
             for t in range(PACK):
                 finish(c, t, cols)
-            group_y(c, cols)
-            if i % 2 == 1:
-                store_y(c, slice(0, PACK), halves[i // 2])
+            if i < 3:
+                group_y(c, cols)
+            if i > 0:
+                store_y(c, slice(0, PACK), halves[0] if i == 1 else cols)
         quantize_y(c, halves[0])
         store_codes(c, halves[0])
+        group_y(c, quarters[3], nc.vector.tensor_copy)
         quantize_y(c, quarters[2])
         quantize_y(c, quarters[3])
         store_codes(c, halves[1])

from contextlib import ExitStack

import concourse.mybir as mybir
from concourse.masks import make_identity

TGT, SRC, F, D = 2048, 1536, 1024, 512
FLOPS = 2 * TGT * SRC * F + 2 * SRC * F * D

F32 = mybir.dt.float32
BF16 = mybir.dt.bfloat16
I32 = mybir.dt.int32
U32 = mybir.dt.uint32
U8 = mybir.dt.uint8
FP4X4 = mybir.dt.float4_e2m1fn_x4
FP8X4 = mybir.dt.float8_e4m3fn_x4
ALU = mybir.AluOpType
ACT = mybir.ActivationFunctionType

P = 128
PACK = 4
CHUNK = P * PACK
NCH = SRC // CHUNK
TP = TGT // CHUNK
FP = F // CHUNK
HALF = CHUNK // 2
HM = HALF // PACK
QUADS = 4


def tile_drift_mass_residual_k5_kernel(
    tc, p_words, p_scales, x_words, x_scales, mass, proj_w, bias, src_feat, point_weight, out_0, out_1, out_2
):
    nc = tc.nc
    with ExitStack() as ctx:
        keep = ctx.enter_context(tc.tile_pool(name="keep", bufs=1))
        work = ctx.enter_context(tc.tile_pool(name="work", bufs=2))
        psum = ctx.enter_context(tc.psum_pool(name="psum", bufs=8))
        ctx.enter_context(tc.manual_schedule())

        def kept(name, shape, dtype):
            return keep.tile(shape, dtype, name=name, align_bytes=256)

        def bank(name):
            return psum.tile([P, CHUNK], F32, name=name, tag="bank")

        x_raw = [kept("x_raw%d" % g, [P, 2 * F], U8) for g in range(TP)]
        x_code = [kept("x_code%d" % g, [P, 2 * F], U8) for g in range(TP)]
        xs_raw = [kept("xs_raw%d" % i, [P, 2, F], U8) for i in range(2)]
        x_scale = [kept("x_scale%d" % g, [P, F], U8) for g in range(TP)]
        first_loads = [slice(0, 1), slice(1, 2), slice(2, TP)]
        p_first = [kept("p_first%d" % gs.start, [P, gs.stop - gs.start, 2 * CHUNK], U8) for gs in first_loads]
        p_rest = [kept("p_rest%d" % c, [P, TP, 2 * CHUNK], U8) for c in range(NCH - 1)]
        ps_first = kept("ps_first", [P, TP, CHUNK], U8)
        ps_rest = kept("ps_rest", [P, TP, SRC - CHUNK], U8)
        w_raw = [kept("w_raw%d" % G, [P, PACK, D], BF16) for G in range(FP)]
        w_group = [kept("w_group%d" % G, [P, D, PACK], BF16) for G in range(FP)]
        w_code = [kept("w_code%d" % G, [P, D], U32) for G in range(FP)]
        w_scale = [kept("w_scale%d" % G, [P, D], U8) for G in range(FP)]
        mass_col = kept("mass_col", [P, NCH * PACK], BF16)
        rmass_col = kept("rmass_col", [P, NCH * PACK], F32)
        rmass = kept("rmass", [P, SRC], F32)
        bias_raw = kept("bias_raw", [P, PACK], BF16)
        weight_raw = kept("weight_raw", [P, NCH, PACK], BF16)
        weight_col = kept("weight_col", [P, NCH * PACK], F32)
        bias_row = kept("bias_row", [P, D], BF16)
        feat = [kept("feat%d" % c, [P, PACK, D], BF16) for c in range(NCH)]
        offset = [kept("offset%d" % t, [P, D], F32) for t in range(PACK)]
        h_code = [[kept("h_code%d_%d" % (c, G), [P, CHUNK], U32) for G in range(FP)] for c in range(NCH)]
        h_scale = [[kept("h_scale%d_%d" % (c, G), [P, CHUNK], U8) for G in range(FP)] for c in range(NCH)]
        y_code = [kept("y_code%d" % c, [P, D], U32) for c in range(NCH)]
        y_scale = [kept("y_scale%d" % c, [P, D], U8) for c in range(NCH)]
        ident = kept("ident", [P, P], F32)

        def p_code(c, g):
            return p_first[min(g, 2)][:, g - min(g, 2), :] if c == 0 else p_rest[c - 1][:, g, :]

        def p_scale(c, g):
            return ps_first[:, g, :] if c == 0 else ps_rest[:, g, (c - 1) * CHUNK : c * CHUNK]

        def load_scale_rows(plane, rows):
            for q in range(QUADS):
                nc.sync.dma_start(
                    out=plane[32 * q : 32 * q + 4, :, :].bitcast(I32),
                    in_=rows[:, 4 * q : 4 * q + 4, :].rearrange("g r n -> r g n").bitcast(I32),
                )

        def load_p_words(dst, gs, c):
            cols = slice(2 * CHUNK * c, 2 * CHUNK * (c + 1))
            nc.sync.dma_start(out=dst[:].bitcast(I32), in_=p_words[gs, :, cols].rearrange("g p n -> p g n").bitcast(I32))

        def load_x_words(g):
            nc.sync.dma_start(out=x_raw[g][:].bitcast(I32), in_=x_words[g].bitcast(I32))

        def load_feat(c):
            rows = src_feat[CHUNK * c : CHUNK * (c + 1), :]
            nc.sync.dma_start(out=feat[c][:], in_=rows.rearrange("(p t) d -> p t d", t=PACK))

        def sort_x_words(g):
            nc.vector.tensor_copy(
                out=x_code[g][:].bitcast(I32).rearrange("p (j q w) -> p j q w", j=8, w=4),
                in_=x_raw[g][:].bitcast(I32).rearrange("p (q j w) -> p j q w", j=8, w=4),
            )

        def sort_x_scales(g):
            nc.vector.tensor_copy(
                out=x_scale[g][:].bitcast(I32).rearrange("p (j q w) -> p j q w", j=8, w=2),
                in_=xs_raw[g // 2][:, g % 2, :].bitcast(I32).rearrange("p (q j w) -> p j q w", j=8, w=2),
            )

        def interleave(engine_copy, dst, src):
            engine_copy(
                out=dst.rearrange("p (c i) t -> p c t i", i=4),
                in_=src.rearrange("p t (c i) -> p c t i", i=4),
            )

        def quantize(codes, scales, grouped):
            nc.vector.quantize_mx(out=codes.bitcast(FP8X4), scales=scales, in_=grouped.rearrange("p n t -> p (n t)"))

        def group_w(G, half, engine_copy):
            cols = slice(HALF * half, HALF * (half + 1))
            interleave(engine_copy, w_group[G][:, cols, :], w_raw[G][:, :, cols])

        def quantize_w(G):
            quantize(w_code[G][:], w_scale[G][:], w_group[G][:])

        sums = {}
        pairs = {}
        h_group = {}
        z_bank = {}
        y_tile = {}
        y_group = {}

        def split(b):
            return b // 4, (b // 2) % 2, b % 2

        def first_pass(c, b, e, g):
            G, half, u = split(b)
            j = PACK * G + 2 * u + e
            if (c, b) not in sums:
                sums[c, b] = bank("sums%d_%d" % (c, b))
            nc.tensor.matmul_mx(
                out=sums[c, b][:, HALF * e : HALF * (e + 1)],
                lhsT=x_code[g][:, 2 * P * j : 2 * P * (j + 1)].bitcast(FP4X4),
                lhsT_scale=x_scale[g][:, P * j : P * (j + 1)],
                rhs=p_code(c, g)[:, 2 * HALF * half : 2 * HALF * (half + 1)].bitcast(FP4X4),
                rhs_scale=p_scale(c, g)[:, HALF * half : HALF * (half + 1)],
                start=(g == 0),
                stop=(g == TP - 1),
            )

        def first_product(c, b):
            for e in range(2):
                for g in range(TP):
                    first_pass(c, b, e, g)

        def divide(c, b, part=slice(0, HALF)):
            G, half, u = split(b)
            s0 = CHUNK * c + HALF * half
            n = part.stop - part.start
            if (c, G, half) not in pairs:
                pairs[c, G, half] = work.tile([P, 2, HALF, 2], BF16, name="pairs", bufs=3, align_bytes=256)
            nc.vector.tensor_tensor(
                out=pairs[c, G, half][:, u, part, :],
                in0=sums[c, b][:].rearrange("p (e s) -> p s e", e=2)[:, part, :],
                in1=rmass[:, s0 + part.start : s0 + part.stop].unsqueeze(2).to_broadcast([P, n, 2]),
                op=ALU.mult,
            )

        def group_h(c, G, half, ms=slice(0, HM)):
            if half == 0:
                h_group[c, G] = work.tile([P, CHUNK, PACK], BF16, name="h_group", bufs=2, align_bytes=256)
            words = h_group[c, G][:].rearrange("p n t -> p (n t)").bitcast(F32)
            nc.scalar.copy(
                out=words.rearrange("p (t h m u) -> p h m t u", t=PACK, h=2, u=2)[:, half, ms, :, :],
                in_=pairs[c, G, half][:].rearrange("p u s e -> p (u s e)").bitcast(F32).rearrange("p (u m t) -> p m t u", u=2, t=PACK)[:, ms, :, :],
            )

        def quantize_h(c, G, parts=1):
            n = CHUNK // parts
            for i in range(parts):
                cols = slice(n * i, n * (i + 1))
                quantize(h_code[c][G][:, cols], h_scale[c][G][:, cols], h_group[c, G][:, cols, :])

        def second_pass(c, t, G, ds=slice(0, D)):
            if G == 0:
                z_bank[c, t, ds.start // HALF] = bank("z%d_%d_%d" % (c, t, ds.start))
                z_bank[c, t, (ds.stop - 1) // HALF] = z_bank[c, t, ds.start // HALF]
            cols = slice(P * t, P * (t + 1))
            nc.tensor.matmul_mx(
                out=z_bank[c, t, ds.start // HALF][:, ds],
                lhsT=h_code[c][G][:, cols].bitcast(FP8X4),
                lhsT_scale=h_scale[c][G][:, cols],
                rhs=w_code[G][:, ds].bitcast(FP8X4),
                rhs_scale=w_scale[G][:, ds],
                start=(G == 0),
                stop=(G == FP - 1),
            )

        def subtract_feat(c, t, cols=slice(0, D)):
            nc.gpsimd.tensor_tensor(out=offset[t][:, cols], in0=bias_row[:, cols], in1=feat[c][:, t, cols], op=ALU.subtract)

        def weigh_offset(c, t):
            k = PACK * c + t
            nc.scalar.activation(out=offset[t][:], in_=offset[t][:], func=ACT.Copy, scale=weight_col[:, k : k + 1])

        def finish(c, t, cols=slice(0, D)):
            if c not in y_tile:
                y_tile[c] = work.tile([P, PACK, D], F32, name="y_tile", bufs=2, align_bytes=256)
                y_group[c] = work.tile([P, D, PACK], BF16, name="y_group", bufs=2, align_bytes=256)
            k = PACK * c + t
            nc.vector.scalar_tensor_tensor(
                out=y_tile[c][:, t, cols],
                in0=z_bank[c, t, cols.start // HALF][:, cols],
                scalar=weight_col[:, k : k + 1],
                in1=offset[t][:, cols],
                op0=ALU.mult,
                op1=ALU.add,
            )

        def store_y(c, ts, cols=slice(0, D)):
            rows = out_0[CHUNK * c : CHUNK * (c + 1), :].rearrange("(p t) d -> p t d", t=PACK)
            nc.sync.dma_start(out=rows[:, ts, cols], in_=y_tile[c][:, ts, cols])

        def group_y(c, cols, engine_copy=nc.scalar.copy):
            interleave(engine_copy, y_group[c][:, cols, :], y_tile[c][:, :, cols])

        def quantize_y(c, cols):
            quantize(y_code[c][:, cols], y_scale[c][:, cols], y_group[c][:, cols, :])

        def store_codes(c, cols=slice(0, D)):
            words = out_1[c].rearrange("p m t -> p (m t)").bitcast(I32)
            nc.sync.dma_start(out=words[:, cols], in_=y_code[c][:, cols].bitcast(I32))

        def store_scales(c, queues=(nc.sync, nc.sync)):
            for q in range(QUADS):
                queues[q % 2].dma_start(
                    out=out_2[c, 4 * q : 4 * q + 4, :].bitcast(I32), in_=y_scale[c][32 * q : 32 * q + 4, :].bitcast(I32)
                )

        def spread(name, dst, columns):
            rows = bank(name)
            n = columns.shape[1]
            for t in range(n):
                nc.tensor.transpose(rows[:, P * t : P * (t + 1)], columns[:, t : t + 1].to_broadcast([P, P]), ident[:])
            nc.scalar.copy(out=dst, in_=rows[:, 0 : P * n].rearrange("p (t m) -> p m t", t=n))

        halves = [slice(0, HALF), slice(HALF, D)]
        quarters = [slice(P * i, P * (i + 1)) for i in range(4)]

        nc.sync.dma_start(out=mass_col[:], in_=mass.rearrange("(p j) -> p j", p=P))
        nc.sync.dma_start(out=bias_raw[:], in_=bias.rearrange("(p t) -> p t", t=PACK))
        load_x_words(0)
        load_p_words(p_first[0], first_loads[0], 0)
        nc.vector.memset(xs_raw[0][:].rearrange("p g n -> p (g n)").bitcast(I32), 0)
        nc.vector.memset(ps_first[:].rearrange("p g n -> p (g n)").bitcast(I32), 0)
        nc.vector.memset(xs_raw[1][:].rearrange("p g n -> p (g n)").bitcast(I32), 0)
        nc.vector.reciprocal(out=rmass_col[:], in_=mass_col[:])
        nc.vector.memset(ps_rest[:].rearrange("p g n -> p (g n)").bitcast(I32), 0)
        make_identity(nc, ident[:])
        nc.gpsimd.dma_start(out=weight_raw[:], in_=point_weight.rearrange("(c p t) -> p c t", p=P, t=PACK))
        load_scale_rows(xs_raw[0], x_scales[0:2])
        load_scale_rows(ps_first, p_scales[:, :, 0:CHUNK])
        load_x_words(1)
        load_p_words(p_first[1], first_loads[1], 0)
        load_scale_rows(xs_raw[1], x_scales[2:4])
        load_x_words(2)
        load_p_words(p_first[2], first_loads[2], 0)
        load_x_words(3)
        w_rows = proj_w.rearrange("(q j r) d -> j q r d", j=8, r=8)
        for j in range(FP * PACK):
            nc.sync.dma_start(out=w_raw[j // PACK][:, j % PACK, :], in_=w_rows[j])
            if j == PACK - 1:
                load_feat(0)
        load_scale_rows(ps_rest, p_scales[:, :, CHUNK:SRC])
        load_p_words(p_rest[0], slice(0, TP), 1)
        load_feat(1)
        load_p_words(p_rest[1], slice(0, TP), 2)
        load_feat(2)

        rmass_runs = rmass[:].rearrange("p (m j) -> p m j", m=P)
        for i in range(NCH):
            js = slice(PACK * i, PACK * (i + 1))
            spread("rmass_rows%d" % i, rmass_runs[:, :, js], rmass_col[:, js])
        spread("bias_rows", bias_row[:].bitcast(F32).rearrange("p (m u) -> p m u", u=2), bias_raw[:].bitcast(F32))
        nc.scalar.activation(out=weight_col[:], in_=weight_raw[:].rearrange("p c t -> p (c t)"), func=ACT.Copy)

        early = 6
        for t in range(PACK):
            for cols in halves:
                subtract_feat(0, t, cols)
        for g in range(TP):
            sort_x_words(g)
            sort_x_scales(g)
            for b in range(early):
                first_pass(0, b, 0, g)
        for half in range(2):
            group_w(0, half, nc.vector.tensor_copy)
        quantize_w(0)
        for b in range(8):
            if b < early:
                for g in range(TP):
                    first_pass(0, b, 1, g)
            else:
                first_product(0, b)
            divide(0, b)
            if b % 2 == 1:
                group_h(0, b // 4, (b // 2) % 2)
            if b in (3, 5):
                group_w(1, (b - 3) // 2, nc.scalar.copy)
        quantize_h(0, 0)
        quantize_w(1)
        quantize_h(0, 1)

        for b in range(8):
            first_product(1, b)
            divide(1, b)
            if b < 2:
                weigh_offset(0, 2 * b)
            if b % 2 == 1:
                group_h(1, b // 4, (b // 2) % 2)
            if b < 2:
                weigh_offset(0, 2 * b + 1)
            t = b - 2
            if t in (1, 2):
                weigh_offset(1, t - 1)
            if 0 <= t < PACK:
                for G in range(FP):
                    second_pass(0, t, G)
                finish(0, t)
                subtract_feat(1, t)
                if t % 2 == 1:
                    store_y(0, slice(t - 1, t + 1))
            if b == 4:
                quantize_h(1, 0)
            if b == 5:
                group_y(0, halves[0])
                weigh_offset(1, 2)
        quantize_y(0, halves[0])
        weigh_offset(1, 3)
        group_y(0, halves[1])
        quantize_h(1, 1)

        for b in range(8):
            first_product(2, b)
            if b == 7:
                for i in range(2):
                    divide(2, b, quarters[i])
                    group_h(2, 1, 1, slice(32 * i, 32 * (i + 1)))
            else:
                divide(2, b)
                if b % 2 == 1:
                    group_h(2, b // 4, (b // 2) % 2)
            t = b - 1
            if t in (1, 2):
                weigh_offset(2, t - 1)
            if 0 <= t < PACK:
                for G in range(FP):
                    second_pass(1, t, G)
                finish(1, t)
                subtract_feat(2, t)
                if t % 2 == 1:
                    store_y(1, slice(t - 1, t + 1))
            if b == 2:
                quantize_y(0, halves[1])
                store_codes(0)
                store_scales(0)
            if b == 4:
                quantize_h(2, 0)
                group_y(1, halves[0])
            if b == 5:
                group_y(1, quarters[2])
            if b == 6:
                group_y(1, quarters[3], nc.vector.tensor_copy)

        c = NCH - 1
        weigh_offset(c, 2)
        weigh_offset(c, 3)
        quantize_y(c - 1, slice(0, D))
        store_codes(c - 1)
        store_scales(c - 1)
        for ds in halves:
            for t in range(PACK):
                second_pass(c, t, 0, ds)
        quantize_h(c, 1, parts=PACK)
        for ds in halves:
            for t in range(PACK):
                second_pass(c, t, 1, ds)
        for i, cols in enumerate(quarters):
            for t in range(PACK):
                finish(c, t, cols)
            if i < 3:
                group_y(c, cols)
            if i > 0:
                store_y(c, slice(0, PACK), halves[0] if i == 1 else cols)
        quantize_y(c, halves[0])
        store_codes(c, halves[0])
        group_y(c, quarters[3], nc.vector.tensor_copy)
        quantize_y(c, quarters[2])
        quantize_y(c, quarters[3])
        store_codes(c, halves[1])
        store_scales(c, (nc.sync, nc.scalar))
